import numpy as np
import ml_dtypes


def mxq(x, axis, fmt="e4m3"):
    dtype, down = {"e4m3": (ml_dtypes.float8_e4m3fn, 7), "e5m2": (ml_dtypes.float8_e5m2, 14)}[fmt]
    v = np.moveaxis(np.asarray(x, np.float32).astype(ml_dtypes.bfloat16).astype(np.float64), axis, -1)
    blocks = v.reshape(v.shape[:-1] + (-1, 32))
    amax = np.abs(blocks).max(-1, keepdims=True)
    byte = np.maximum(np.where(amax > 0, np.frexp(amax)[1] - 1 + 127, 0) - down, 1)
    scale = np.exp2(byte - 127.0)
    codes = (blocks / scale).astype(np.float32).astype(dtype).astype(np.float64)
    return np.moveaxis((codes * scale).reshape(v.shape), -1, axis)


WIDE = False


def mx_kscale(k):
    if not WIDE:
        return np.ones(k)
    levels = np.array([10, -10, 5, -5, 0])
    if k % 512:
        return np.exp2(np.random.permutation(np.resize(levels, k // 32))).repeat(32)
    a = np.empty((k // 512, 16))
    for p in range(k // 512):
        a[p, :8] = np.random.permutation(np.resize(levels, 8))
        for g in range(8):
            far = levels[np.abs(levels - a[p, g]) >= 10]
            a[p, g + 8] = far[np.random.randint(len(far))]
    return np.exp2(a.ravel()).repeat(32)


def f64(x):
    return np.asarray(x).astype(np.float64)


def striped(idx):
    return np.tile(idx.reshape(-1, 16).T, (8, 1)).astype(np.uint16)


def unstriped(offs):
    return offs[:16].T.reshape(-1).astype(np.int64)


def striped8(idx):
    return np.concatenate([x.reshape(-1, 16).T for x in idx]).astype(np.uint16)


def runs(offs, k):
    lists = np.stack([offs[16 * r : 16 * r + 16].T.reshape(-1) for r in range(8)]).astype(np.int64)
    return lists[np.arange(k) % 512 // 64]


def pack_weight(w):
    k, n = w.shape
    w = f64(np.asarray(w, np.float32).astype(ml_dtypes.bfloat16)).reshape(k // 32, 32, n)
    amax = np.abs(w).max(1)
    byte = np.clip(np.where(amax > 0, np.frexp(amax)[1] - 1 + 127 - 7, 1), 1, 254)
    scaled = (w * np.exp2(127.0 - byte)[:, None, :]).reshape(k, n).astype(np.float32)
    words = np.ascontiguousarray(scaled.reshape(k // 512, 128, 4, n).transpose(0, 1, 3, 2)).astype(ml_dtypes.float8_e4m3fn).view(np.uint8)
    return words, np.ascontiguousarray(byte.astype(np.uint8).reshape(k // 512, 16, n))


def unpack_weight(words, scales):
    g, p, n, _ = words.shape
    vals = np.ascontiguousarray(words).view(ml_dtypes.float8_e4m3fn).astype(np.float64) * np.repeat(np.exp2(scales.astype(np.float64) - 127.0), 8, axis=1)[..., None]
    return vals.transpose(0, 1, 3, 2).reshape(g * 512, n)


def relu(v):
    return np.maximum(v, 0.0)


K, T, S, H, C = 512, 2048, 512, 512, 512


def setup_inputs():
    n = np.random.standard_normal
    s = mx_kscale(K)[:, None]
    packed_xT = pack_weight(n((K, T)) * s)
    return {
        "x_words": packed_xT[0],
        "x_scales": packed_xT[1],
        "w1": (n((K, H)) / np.sqrt(K) / s).astype(np.float32),
        "gs": (np.random.uniform(0.5, 1.5, (K, 1)) / s).astype(np.float32),
        "offs": striped(np.random.permutation(T)[:S]),
        "cand": striped(np.random.permutation(T)[:C]),
        "n1": striped8(np.stack([np.random.permutation(S) for _ in range(8)])),
        "n2": striped8(np.stack([np.random.permutation(S) for _ in range(8)])),
        "n3": striped8(np.stack([np.random.permutation(S) for _ in range(8)])),
    }


def reference(x_words, x_scales, w1, gs, offs, cand, n1, n2, n3):
    x_cand = unpack_weight(x_words, x_scales)[:, unstriped(cand)]
    xq = unpack_weight(x_words, x_scales)[:, unstriped(offs)]
    h = relu(mxq(f64(w1), 0, "e4m3").T @ xq)
    z = f64(gs) * h
    s = 0.0625 * ((x_cand.T @ mxq(z, 0, "e4m3")))
    ex = np.exp(0.5 * s)
    return np.log((ex + ex[np.arange(C)[:, None], runs(n1, C)]) / (ex[np.arange(C)[:, None], runs(n2, C)] + ex[np.arange(C)[:, None], runs(n3, C)]))

@@ -1,0 +1,196 @@
+from contextlib import ExitStack
+
+import concourse.mybir as mybir
+
+K, T, S, H, C = 512, 2048, 512, 512, 512
+FLOPS = 2 * K * H * S + 2 * H * C * S
+
+F32 = mybir.dt.float32
+BF16 = mybir.dt.bfloat16
+I32 = mybir.dt.int32
+U32 = mybir.dt.uint32
+U16 = mybir.dt.uint16
+U8 = mybir.dt.uint8
+FP8X4 = mybir.dt.float8_e4m3fn_x4
+ALU = mybir.AluOpType
+ACT = mybir.ActivationFunctionType
+
+P = 128
+PACK = 4
+CHUNK = 128
+HALF = 256
+WINDOW = 1024
+EXP_SCALE = 0.5 * 0.0625
+
+
+def tile_picked_candodds_none_p_kernel(
+    tc, x_words, x_scales, w1, gs, offs, cand, n1, n2, n3, out
+):
+    nc = tc.nc
+    with ExitStack() as ctx:
+        keep = ctx.enter_context(tc.tile_pool(name="keep", bufs=1))
+        psum = ctx.enter_context(tc.psum_pool(name="psum", bufs=1))
+
+        def sbuf(name, shape, dtype):
+            return keep.tile(shape, dtype, name=name, align_bytes=64)
+
+        table_words = sbuf("table_words", [P, T], I32)
+        table_scales = sbuf("table_scales", [P, T], U8)
+        offs_sb = sbuf("offs_sb", [P, S // 16], U16)
+        cand_sb = sbuf("cand_sb", [P, C // 16], U16)
+        n1_sb = sbuf("n1_sb", [P, S // 16], U16)
+        n2_sb = sbuf("n2_sb", [P, S // 16], U16)
+        n3_sb = sbuf("n3_sb", [P, S // 16], U16)
+        w_raw = [sbuf("w_raw%d" % a, [P, PACK, HALF], F32) for a in range(2)]
+        gs_sb = sbuf("gs_sb", [P, PACK], F32)
+
+        nc.vector.memset(table_scales[:].bitcast(I32), 0)
+        nc.sync.dma_start(out=table_words[:], in_=x_words[0].rearrange("p n t -> p (n t)").bitcast(I32))
+        for q in range(4):
+            nc.sync.dma_start(
+                out=table_scales[32 * q : 32 * q + 4, :].bitcast(I32),
+                in_=x_scales[0, 4 * q : 4 * q + 4, :].bitcast(I32),
+            )
+        nc.sync.dma_start(offs_sb[:], offs)
+        nc.sync.dma_start(cand_sb[:], cand)
+        w_rows = w1.rearrange("(p j) c -> p j c", j=PACK)
+        for a in range(2):
+            nc.sync.dma_start(out=w_raw[a][:], in_=w_rows[:, :, a * HALF : (a + 1) * HALF])
+        nc.sync.dma_start(out=gs_sb[:], in_=gs.rearrange("(p t) o -> p (t o)", t=PACK))
+        nc.sync.dma_start(n2_sb[:], n2)
+        nc.sync.dma_start(n3_sb[:], n3)
+        nc.sync.dma_start(n1_sb[:], n1)
+
+        ex = [sbuf("ex%d" % t, [P, WINDOW], F32) for t in range(PACK)]
+        score = {t: sbuf("score%d" % t, [P, WINDOW], F32) for t in range(1, PACK)}
+        for window in ex + list(score.values()):
+            nc.vector.memset(window[:, S:], 0.0)
+        warm = sbuf("warm", [P, 1], F32)
+        nc.scalar.activation(out=warm[:], in_=ex[0][:, S : S + 1], func=ACT.Exp)
+
+        w_grouped = keep.tile([P, PACK, P, PACK], BF16, name="w_grouped", tag="after_w", align_bytes=64)
+        for a in range(2):
+            nc.scalar.copy(
+                out=w_grouped[:, :, 64 * a : 64 * (a + 1), :].rearrange("p t m j -> p m t j"),
+                in_=w_raw[a][:].rearrange("p j (m t) -> p m t j", t=PACK),
+            )
+
+        tok_words = sbuf("tok_words", [P, S], U32)
+        tok_scales = sbuf("tok_scales", [P, S], U8)
+        cand_words = sbuf("cand_words", [P, C], U32)
+        dealt_words = sbuf("dealt_words", [P, PACK, P], U32)
+        dealt_scales = sbuf("dealt_scales", [P, PACK, P], U8)
+        w_codes = sbuf("w_codes", [P, H], U32)
+        w_scales = sbuf("w_scales", [P, H], U8)
+
+        words_window = table_words[:].bitcast(U32)
+        nc.vector.tensor_copy(tok_words[:], words_window.indirect(offs_sb[:]))
+        nc.vector.tensor_copy(tok_scales[:], table_scales[:].indirect(offs_sb[:]))
+        nc.vector.tensor_copy(cand_words[:], words_window.indirect(cand_sb[:]))
+        nc.vector.quantize_mx(
+            out=w_codes[:].bitcast(FP8X4), scales=w_scales[:], in_=w_grouped[:].rearrange("p t m j -> p (t m j)")
+        )
+        cand_scales = keep.tile([P, C], U8, name="cand_scales", tag="after_w", align_bytes=64)
+        nc.vector.tensor_copy(cand_scales[:], table_scales[:].indirect(cand_sb[:]))
+        nc.vector.tensor_copy(dealt_words[:], cand_words[:].rearrange("p (m t) -> p t m", t=PACK))
+        nc.vector.tensor_copy(dealt_scales[:], cand_scales[:].rearrange("p (m t) -> p t m", t=PACK))
+
+        hidden = [psum.tile([P, PACK, CHUNK], F32, name="hidden%d" % c) for c in range(4)]
+        for c in range(4):
+            cols = slice(c * CHUNK, (c + 1) * CHUNK)
+            for t in range(PACK):
+                nc.tensor.matmul_mx(
+                    out=hidden[c][:, t, :],
+                    lhsT=w_codes[:, t * P : (t + 1) * P].bitcast(FP8X4),
+                    lhsT_scale=w_scales[:, t * P : (t + 1) * P],
+                    rhs=tok_words[:, cols].bitcast(FP8X4),
+                    rhs_scale=tok_scales[:, cols],
+                    start=True,
+                    stop=True,
+                )
+
+        z = [sbuf("z%d" % c, [P, CHUNK, PACK], BF16) for c in range(4)]
+        z_codes = [sbuf("z_codes%d" % h, [P, HALF], U32) for h in range(2)]
+        z_scales = [sbuf("z_scales%d" % h, [P, HALF], U8) for h in range(2)]
+        gs_spread = gs_sb[:].unsqueeze(1).to_broadcast([P, CHUNK, PACK])
+
+        def weigh(c):
+            nc.vector.scalar_tensor_tensor(
+                out=z[c][:],
+                in0=hidden[c][:].rearrange("p t n -> p n t"),
+                scalar=0.0,
+                in1=gs_spread,
+                op0=ALU.max,
+                op1=ALU.mult,
+            )
+
+        def quantize_z(c):
+            cols = slice((c % 2) * CHUNK, (c % 2 + 1) * CHUNK)
+            nc.vector.quantize_mx(
+                out=z_codes[c // 2][:, cols].bitcast(FP8X4),
+                scales=z_scales[c // 2][:, cols],
+                in_=z[c][:].rearrange("p n t -> p (n t)"),
+            )
+
+        sums = [[psum.tile([P, 2, HALF], F32, name="sums%d%d" % (h, u)) for u in range(2)] for h in range(2)]
+        ex_copy = [[sbuf("ex_copy%d" % t, [P, S], F32)] for t in range(PACK)]
+
+        def scores(h):
+            for t in range(PACK):
+                nc.tensor.matmul_mx(
+                    out=sums[h][t // 2][:, t % 2, :],
+                    lhsT=dealt_words[:, t, :].bitcast(FP8X4),
+                    lhsT_scale=dealt_scales[:, t, :],
+                    rhs=z_codes[h][:].bitcast(FP8X4),
+                    rhs_scale=z_scales[h][:],
+                    start=True,
+                    stop=True,
+                )
+
+        def exponentiate(h, t):
+            cols = slice(h * HALF, (h + 1) * HALF)
+            nc.scalar.activation(out=ex[t][:, cols], in_=sums[h][t // 2][:, t % 2, :], func=ACT.Exp, scale=EXP_SCALE)
+            nc.sync.dma_start(out=ex_copy[t][0][:, cols], in_=ex[t][:, cols])
+
+        weigh(0)
+        weigh(1)
+        quantize_z(0)
+        weigh(2)
+        quantize_z(1)
+        scores(0)
+        weigh(3)
+        quantize_z(2)
+        quantize_z(3)
+        for t in range(PACK):
+            exponentiate(0, t)
+        scores(1)
+        for t in range(1, PACK):
+            nc.vector.tensor_copy(score[t][:, :HALF], sums[0][t // 2][:, t % 2, :])
+
+        at_n2 = [sbuf("at_n2_%d" % t, [P, S], F32) for t in range(PACK)]
+        for t in range(PACK):
+            exponentiate(1, t)
+            if t == 0:
+                nc.vector.tensor_copy(at_n2[t][:], ex[t][:].indirect(n2_sb[:]))
+            else:
+                nc.scalar.copy(out=score[t][:, HALF:S], in_=sums[1][t // 2][:, t % 2, :])
+                nc.scalar.activation(out=at_n2[t][:], in_=score[t][:].indirect(n2_sb[:]), func=ACT.Exp, scale=EXP_SCALE)
+
+        out_rows = out.rearrange("(p t) n -> p t n", t=PACK)
+        pieces = [(t, 0, S) for t in range(PACK - 1)] + [(PACK - 1, 0, HALF), (PACK - 1, HALF, S)]
+        pairs = []
+        for t, lo, hi in pieces:
+            pair = sbuf("pair%d_%d" % (t, lo), [P, 2, hi - lo], F32)
+            entries = slice(lo // 16, hi // 16)
+            steps = [(0, n1_sb, ex_copy[t][0]), (1, n3_sb, at_n2[t])]
+            if t == 0:
+                steps = steps[::-1]
+            for side, places, plain in steps:
+                nc.vector.tensor_tensor(pair[:, side, :], ex[t][:].indirect(places[:, entries]), plain[:, lo:hi], ALU.add)
+            pairs.append(pair)
+        for (t, lo, hi), pair in zip(pieces, pairs):
+            logs = sbuf("logs%d_%d" % (t, lo), [P, 2, hi - lo], F32)
+            nc.scalar.activation(out=logs[:], in_=pair[:], func=ACT.Ln)
+            odds = sbuf("odds%d_%d" % (t, lo), [P, hi - lo], F32)
+            nc.vector.tensor_tensor(odds[:], logs[:, 0, :], logs[:, 1, :], ALU.subtract)
+            nc.sync.dma_start(out=out_rows[:, t, lo:hi], in_=odds[:])

@@ -46,16 +46,16 @@ def tile_picked_candodds_none_p_kernel(
 
         nc.vector.memset(table_scales[:].bitcast(I32), 0)
         nc.sync.dma_start(out=table_words[:], in_=x_words[0].rearrange("p n t -> p (n t)").bitcast(I32))
+        nc.sync.dma_start(offs_sb[:], offs)
+        nc.sync.dma_start(cand_sb[:], cand)
+        w_rows = w1.rearrange("(p j) c -> p j c", j=PACK)
+        nc.sync.dma_start(out=w_raw[0][:], in_=w_rows[:, :, :HALF])
         for q in range(4):
             nc.sync.dma_start(
                 out=table_scales[32 * q : 32 * q + 4, :].bitcast(I32),
                 in_=x_scales[0, 4 * q : 4 * q + 4, :].bitcast(I32),
             )
-        nc.sync.dma_start(offs_sb[:], offs)
-        nc.sync.dma_start(cand_sb[:], cand)
-        w_rows = w1.rearrange("(p j) c -> p j c", j=PACK)
-        for a in range(2):
-            nc.sync.dma_start(out=w_raw[a][:], in_=w_rows[:, :, a * HALF : (a + 1) * HALF])
+        nc.sync.dma_start(out=w_raw[1][:], in_=w_rows[:, :, HALF:])
         nc.sync.dma_start(out=gs_sb[:], in_=gs.rearrange("(p t) o -> p (t o)", t=PACK))
         nc.sync.dma_start(n2_sb[:], n2)
         nc.sync.dma_start(n3_sb[:], n3)
@@ -71,8 +71,8 @@ def tile_picked_candodds_none_p_kernel(
         w_grouped = keep.tile([P, PACK, P, PACK], BF16, name="w_grouped", tag="after_w", align_bytes=64)
         for a in range(2):
             nc.scalar.copy(
-                out=w_grouped[:, :, 64 * a : 64 * (a + 1), :].rearrange("p t m j -> p m t j"),
-                in_=w_raw[a][:].rearrange("p j (m t) -> p m t j", t=PACK),
+                out=w_grouped[:, :, 64 * a : 64 * (a + 1), :].rearrange("p t m j -> p m j t"),
+                in_=w_raw[a][:].rearrange("p j (m t) -> p m j t", t=PACK),
             )
 
         tok_words = sbuf("tok_words", [P, S], U32)
@@ -85,8 +85,8 @@ def tile_picked_candodds_none_p_kernel(
 
         words_window = table_words[:].bitcast(U32)
         nc.vector.tensor_copy(tok_words[:], words_window.indirect(offs_sb[:]))
-        nc.vector.tensor_copy(tok_scales[:], table_scales[:].indirect(offs_sb[:]))
         nc.vector.tensor_copy(cand_words[:], words_window.indirect(cand_sb[:]))
+        nc.vector.tensor_copy(tok_scales[:], table_scales[:].indirect(offs_sb[:]))
         nc.vector.quantize_mx(
             out=w_codes[:].bitcast(FP8X4), scales=w_scales[:], in_=w_grouped[:].rearrange("p t m j -> p (t m j)")
         )
@@ -96,7 +96,7 @@ def tile_picked_candodds_none_p_kernel(
         nc.vector.tensor_copy(dealt_scales[:], cand_scales[:].rearrange("p (m t) -> p t m", t=PACK))
 
         hidden = [psum.tile([P, PACK, CHUNK], F32, name="hidden%d" % c) for c in range(4)]
-        for c in range(4):
+        for c in (2, 0, 1, 3):
             cols = slice(c * CHUNK, (c + 1) * CHUNK)
             for t in range(PACK):
                 nc.tensor.matmul_mx(
@@ -109,14 +109,15 @@ def tile_picked_candodds_none_p_kernel(
                     stop=True,
                 )
 
-        z = [sbuf("z%d" % c, [P, CHUNK, PACK], BF16) for c in range(4)]
+        z = [sbuf("z%d" % c, [P, CHUNK, PACK], BF16)[:] for c in (0, 1, 3)]
+        z.insert(2, score[1][:, :HALF].bitcast(BF16).rearrange("p (n t) -> p n t", t=PACK))
         z_codes = [sbuf("z_codes%d" % h, [P, HALF], U32) for h in range(2)]
         z_scales = [sbuf("z_scales%d" % h, [P, HALF], U8) for h in range(2)]
         gs_spread = gs_sb[:].unsqueeze(1).to_broadcast([P, CHUNK, PACK])
 
         def weigh(c):
             nc.vector.scalar_tensor_tensor(
-                out=z[c][:],
+                out=z[c],
                 in0=hidden[c][:].rearrange("p t n -> p n t"),
                 scalar=0.0,
                 in1=gs_spread,
@@ -124,73 +125,104 @@ def tile_picked_candodds_none_p_kernel(
                 op1=ALU.mult,
             )
 
+        def weigh_on_scalar(c):
+            positive = sbuf("positive", [P, PACK, CHUNK], F32)
+            nc.scalar.activation(out=positive[:], in_=hidden[c][:], func=ACT.Relu)
+            planes = score[2][:, :HALF].bitcast(BF16).rearrange("p (t n) -> p t n", t=PACK)
+            for t in range(PACK):
+                nc.scalar.activation(out=planes[:, t, :], in_=positive[:, t, :], func=ACT.Copy, scale=gs_sb[:, t : t + 1])
+            nc.scalar.copy(
+                out=z[c].rearrange("p (g i) t -> p g t i", i=4), in_=planes.rearrange("p t (g i) -> p g t i", i=4)
+            )
+
         def quantize_z(c):
             cols = slice((c % 2) * CHUNK, (c % 2 + 1) * CHUNK)
             nc.vector.quantize_mx(
                 out=z_codes[c // 2][:, cols].bitcast(FP8X4),
                 scales=z_scales[c // 2][:, cols],
-                in_=z[c][:].rearrange("p n t -> p (n t)"),
+                in_=z[c].rearrange("p n t -> p (n t)"),
             )
 
-        sums = [[psum.tile([P, 2, HALF], F32, name="sums%d%d" % (h, u)) for u in range(2)] for h in range(2)]
-        ex_copy = [[sbuf("ex_copy%d" % t, [P, S], F32)] for t in range(PACK)]
+        last = PACK - 1
+        pairs = [sbuf("pair%d" % t, [P, 2, S], F32) for t in range(PACK)]
+        ex_copy = [pairs[t + 2][:, 1, :] for t in range(2)] + [sbuf("ex_copy%d" % t, [P, S], F32)[:] for t in (2, 3)]
+        at_n2 = [
+            keep.tile([P, S], F32, name="at_n2_%d" % t, tag="at_n2_%d" % t, align_bytes=64) for t in range(PACK)
+        ]
+        shared = psum.tile([P, 2, HALF], F32, name="shared")
+        sums = {(1, 0): shared[:, 0, :], (0, last): shared[:, 1, :]}
 
-        def scores(h):
-            for t in range(PACK):
-                nc.tensor.matmul_mx(
-                    out=sums[h][t // 2][:, t % 2, :],
-                    lhsT=dealt_words[:, t, :].bitcast(FP8X4),
-                    lhsT_scale=dealt_scales[:, t, :],
-                    rhs=z_codes[h][:].bitcast(FP8X4),
-                    rhs_scale=z_scales[h][:],
-                    start=True,
-                    stop=True,
-                )
+        def scores(h, t):
+            if (h, t) not in sums:
+                tag = "sums%d" % t if h == 0 else "hidden%d" % (t - 1)
+                sums.setdefault((h, t), psum.tile([P, HALF], F32, name="sums%d%d" % (h, t), tag=tag)[:])
+            nc.tensor.matmul_mx(
+                out=sums[(h, t)],
+                lhsT=dealt_words[:, t, :].bitcast(FP8X4),
+                lhsT_scale=dealt_scales[:, t, :],
+                rhs=z_codes[h][:].bitcast(FP8X4),
+                rhs_scale=z_scales[h][:],
+                start=True,
+                stop=True,
+            )
 
         def exponentiate(h, t):
             cols = slice(h * HALF, (h + 1) * HALF)
-            nc.scalar.activation(out=ex[t][:, cols], in_=sums[h][t // 2][:, t % 2, :], func=ACT.Exp, scale=EXP_SCALE)
-            nc.sync.dma_start(out=ex_copy[t][0][:, cols], in_=ex[t][:, cols])
+            nc.scalar.activation(out=ex[t][:, cols], in_=sums[(h, t)], func=ACT.Exp, scale=EXP_SCALE)
+            nc.sync.dma_start(out=ex_copy[t][:, cols], in_=ex[t][:, cols])
 
+        def fetch_n2_on_scalar(t):
+            nc.scalar.copy(out=score[t][:, HALF:S], in_=sums[(1, t)])
+            nc.scalar.activation(out=at_n2[t][:], in_=score[t][:].indirect(n2_sb[:]), func=ACT.Exp, scale=EXP_SCALE)
+
+        weigh_on_scalar(2)
         weigh(0)
         weigh(1)
         quantize_z(0)
-        weigh(2)
         quantize_z(1)
-        scores(0)
+        for t in range(last):
+            scores(0, t)
         weigh(3)
         quantize_z(2)
         quantize_z(3)
-        for t in range(PACK):
+        for t in range(last):
             exponentiate(0, t)
-        scores(1)
-        for t in range(1, PACK):
-            nc.vector.tensor_copy(score[t][:, :HALF], sums[0][t // 2][:, t % 2, :])
-
-        at_n2 = [sbuf("at_n2_%d" % t, [P, S], F32) for t in range(PACK)]
         for t in range(PACK):
-            exponentiate(1, t)
-            if t == 0:
-                nc.vector.tensor_copy(at_n2[t][:], ex[t][:].indirect(n2_sb[:]))
-            else:
-                nc.scalar.copy(out=score[t][:, HALF:S], in_=sums[1][t // 2][:, t % 2, :])
-                nc.scalar.activation(out=at_n2[t][:], in_=score[t][:].indirect(n2_sb[:]), func=ACT.Exp, scale=EXP_SCALE)
+            scores(1, t)
+        for t in (1, 2):
+            nc.vector.tensor_copy(score[t][:, :HALF], sums[(0, t)])
+        exponentiate(1, 0)
+        scores(0, last)
+        nc.vector.tensor_copy(at_n2[0][:], ex[0][:].indirect(n2_sb[:]))
+        exponentiate(1, 1)
+        fetch_n2_on_scalar(1)
+        exponentiate(1, 2)
+        exponentiate(0, last)
+        exponentiate(1, last)
+        fetch_n2_on_scalar(2)
+        nc.scalar.copy(out=score[last][:, :HALF], in_=sums[(0, last)])
+        fetch_n2_on_scalar(last)
+
+        def numerator(t):
+            nc.vector.tensor_tensor(pairs[t][:, 0, :], ex[t][:].indirect(n1_sb[:]), ex_copy[t], ALU.add)
+
+        def denominator(t):
+            nc.vector.tensor_tensor(pairs[t][:, 1, :], ex[t][:].indirect(n3_sb[:]), at_n2[t][:], ALU.add)
+
+        denominator(0)
+        denominator(1)
+        numerator(0)
+        numerator(1)
+        for t in range(2, PACK):
+            denominator(t)
+            numerator(t)
 
         out_rows = out.rearrange("(p t) n -> p t n", t=PACK)
-        pieces = [(t, 0, S) for t in range(PACK - 1)] + [(PACK - 1, 0, HALF), (PACK - 1, HALF, S)]
-        pairs = []
+        pieces = [(t, 0, S) for t in range(last)] + [(last, 0, HALF), (last, HALF, S)]
         for t, lo, hi in pieces:
-            pair = sbuf("pair%d_%d" % (t, lo), [P, 2, hi - lo], F32)
-            entries = slice(lo // 16, hi // 16)
-            steps = [(0, n1_sb, ex_copy[t][0]), (1, n3_sb, at_n2[t])]
-            if t == 0:
-                steps = steps[::-1]
-            for side, places, plain in steps:
-                nc.vector.tensor_tensor(pair[:, side, :], ex[t][:].indirect(places[:, entries]), plain[:, lo:hi], ALU.add)
-            pairs.append(pair)
-        for (t, lo, hi), pair in zip(pieces, pairs):
             logs = sbuf("logs%d_%d" % (t, lo), [P, 2, hi - lo], F32)
-            nc.scalar.activation(out=logs[:], in_=pair[:], func=ACT.Ln)
-            odds = sbuf("odds%d_%d" % (t, lo), [P, hi - lo], F32)
+            nc.scalar.activation(out=logs[:], in_=pairs[t][:, :, lo:hi], func=ACT.Ln)
+            tag = "at_n2_%d" % last if t == 0 else "odds%d_%d" % (t, lo)
+            odds = keep.tile([P, hi - lo], F32, name="odds%d_%d" % (t, lo), tag=tag, align_bytes=64)
             nc.vector.tensor_tensor(odds[:], logs[:, 0, :], logs[:, 1, :], ALU.subtract)
             nc.sync.dma_start(out=out_rows[:, t, lo:hi], in_=odds[:])

@@ -41,7 +41,11 @@ def tile_picked_candodds_none_p_kernel(
         n1_sb = sbuf("n1_sb", [P, S // 16], U16)
         n2_sb = sbuf("n2_sb", [P, S // 16], U16)
         n3_sb = sbuf("n3_sb", [P, S // 16], U16)
-        w_raw = [sbuf("w_raw%d" % a, [P, PACK, HALF], F32) for a in range(2)]
+        w_parts = [(0, 256), (256, 384), (384, 512)]
+        spare = [S, S, PACK * 256, PACK * 128]
+        ex = [sbuf("ex%d" % t, [P, S + spare[t]], F32) for t in range(PACK)]
+        w_raw = [ex[a + 2][:, S:].rearrange("p (j c) -> p j c", j=PACK) for a in range(2)]
+        w_raw.append(keep.tile([P, PACK, 128], F32, name="w_last", tag="after_cast", align_bytes=64)[:])
         gs_sb = sbuf("gs_sb", [P, PACK], F32)
 
         nc.vector.memset(table_scales[:].bitcast(I32), 0)
@@ -49,36 +53,35 @@ def tile_picked_candodds_none_p_kernel(
         nc.sync.dma_start(offs_sb[:], offs)
         nc.sync.dma_start(cand_sb[:], cand)
         w_rows = w1.rearrange("(p j) c -> p j c", j=PACK)
-        nc.sync.dma_start(out=w_raw[0][:], in_=w_rows[:, :, :HALF])
+        nc.sync.dma_start(out=w_raw[0], in_=w_rows[:, :, :HALF])
         for q in range(4):
             nc.sync.dma_start(
                 out=table_scales[32 * q : 32 * q + 4, :].bitcast(I32),
                 in_=x_scales[0, 4 * q : 4 * q + 4, :].bitcast(I32),
             )
-        nc.sync.dma_start(out=w_raw[1][:], in_=w_rows[:, :, HALF:])
+        for a in (1, 2):
+            nc.sync.dma_start(out=w_raw[a], in_=w_rows[:, :, w_parts[a][0] : w_parts[a][1]])
         nc.sync.dma_start(out=gs_sb[:], in_=gs.rearrange("(p t) o -> p (t o)", t=PACK))
         nc.sync.dma_start(n2_sb[:], n2)
         nc.sync.dma_start(n3_sb[:], n3)
         nc.sync.dma_start(n1_sb[:], n1)
 
-        ex = [sbuf("ex%d" % t, [P, WINDOW], F32) for t in range(PACK)]
         score = {t: sbuf("score%d" % t, [P, WINDOW], F32) for t in range(1, PACK)}
-        for window in ex + list(score.values()):
+        for window in (ex[0], ex[1], score[1], score[2]):
             nc.vector.memset(window[:, S:], 0.0)
         warm = sbuf("warm", [P, 1], F32)
         nc.scalar.activation(out=warm[:], in_=ex[0][:, S : S + 1], func=ACT.Exp)
 
         w_grouped = keep.tile([P, PACK, P, PACK], BF16, name="w_grouped", tag="after_w", align_bytes=64)
-        for a in range(2):
+        for a, (lo, hi) in enumerate(w_parts):
             nc.scalar.copy(
-                out=w_grouped[:, :, 64 * a : 64 * (a + 1), :].rearrange("p t m j -> p m j t"),
-                in_=w_raw[a][:].rearrange("p j (m t) -> p m j t", t=PACK),
+                out=w_grouped[:, :, lo // PACK : hi // PACK, :].rearrange("p t m j -> p m j t"),
+                in_=w_raw[a].rearrange("p j (m t) -> p m j t", t=PACK),
             )
 
         tok_words = sbuf("tok_words", [P, S], U32)
         tok_scales = sbuf("tok_scales", [P, S], U8)
         cand_words = sbuf("cand_words", [P, C], U32)
-        dealt_words = sbuf("dealt_words", [P, PACK, P], U32)
         dealt_scales = sbuf("dealt_scales", [P, PACK, P], U8)
         w_codes = sbuf("w_codes", [P, H], U32)
         w_scales = sbuf("w_scales", [P, H], U8)
@@ -90,10 +93,14 @@ def tile_picked_candodds_none_p_kernel(
         nc.vector.quantize_mx(
             out=w_codes[:].bitcast(FP8X4), scales=w_scales[:], in_=w_grouped[:].rearrange("p t m j -> p (t m j)")
         )
-        cand_scales = keep.tile([P, C], U8, name="cand_scales", tag="after_w", align_bytes=64)
+        cand_scales = keep.tile([P, C], U8, name="cand_scales", tag="after_cast", align_bytes=64)
         nc.vector.tensor_copy(cand_scales[:], table_scales[:].indirect(cand_sb[:]))
-        nc.vector.tensor_copy(dealt_words[:], cand_words[:].rearrange("p (m t) -> p t m", t=PACK))
-        nc.vector.tensor_copy(dealt_scales[:], cand_scales[:].rearrange("p (m t) -> p t m", t=PACK))
+        dealt_words = keep.tile([P, PACK, P], U32, name="dealt_words", tag="after_w", align_bytes=64)
+        for dealt, picked, run in ((dealt_words, cand_words, 4), (dealt_scales, cand_scales, 16)):
+            nc.vector.tensor_copy(
+                dealt[:].rearrange("p t (g i) -> p g t i", i=run),
+                picked[:].rearrange("p (g i t) -> p g t i", i=run, t=PACK),
+            )
 
         hidden = [psum.tile([P, PACK, CHUNK], F32, name="hidden%d" % c) for c in range(4)]
         for c in (2, 0, 1, 3):
@@ -109,8 +116,8 @@ def tile_picked_candodds_none_p_kernel(
                     stop=True,
                 )
 
-        z = [sbuf("z%d" % c, [P, CHUNK, PACK], BF16)[:] for c in (0, 1, 3)]
-        z.insert(2, score[1][:, :HALF].bitcast(BF16).rearrange("p (n t) -> p n t", t=PACK))
+        z = [sbuf("z%d" % c, [P, CHUNK, PACK], BF16)[:] for c in (0, 1)]
+        z.extend([score[1][:, :HALF].bitcast(BF16).rearrange("p (n t) -> p n t", t=PACK), z[0]])
         z_codes = [sbuf("z_codes%d" % h, [P, HALF], U32) for h in range(2)]
         z_scales = [sbuf("z_scales%d" % h, [P, HALF], U8) for h in range(2)]
         gs_spread = gs_sb[:].unsqueeze(1).to_broadcast([P, CHUNK, PACK])
@@ -126,8 +133,8 @@ def tile_picked_candodds_none_p_kernel(
             )
 
         def weigh_on_scalar(c):
-            positive = sbuf("positive", [P, PACK, CHUNK], F32)
-            nc.scalar.activation(out=positive[:], in_=hidden[c][:], func=ACT.Relu)
+            positive = score[PACK - 1][:, S:].rearrange("p (t n) -> p t n", t=PACK)
+            nc.scalar.activation(out=positive, in_=hidden[c][:], func=ACT.Relu)
             planes = score[2][:, :HALF].bitcast(BF16).rearrange("p (t n) -> p t n", t=PACK)
             for t in range(PACK):
                 nc.scalar.activation(out=planes[:, t, :], in_=positive[:, t, :], func=ACT.Copy, scale=gs_sb[:, t : t + 1])
@@ -193,7 +200,8 @@ def tile_picked_candodds_none_p_kernel(
             nc.vector.tensor_copy(score[t][:, :HALF], sums[(0, t)])
         exponentiate(1, 0)
         scores(0, last)
-        nc.vector.tensor_copy(at_n2[0][:], ex[0][:].indirect(n2_sb[:]))
+        for h in range(2):
+            nc.vector.tensor_copy(at_n2[0][:, h * HALF : (h + 1) * HALF], ex[0][:].indirect(n2_sb[:, 16 * h : 16 * (h + 1)]))
         exponentiate(1, 1)
         fetch_n2_on_scalar(1)
         exponentiate(1, 2)
@@ -209,7 +217,11 @@ def tile_picked_candodds_none_p_kernel(
         def denominator(t):
             nc.vector.tensor_tensor(pairs[t][:, 1, :], ex[t][:].indirect(n3_sb[:]), at_n2[t][:], ALU.add)
 
-        denominator(0)
+        for h in range(2):
+            cols = slice(h * HALF, (h + 1) * HALF)
+            nc.vector.tensor_tensor(
+                pairs[0][:, 1, cols], ex[0][:].indirect(n3_sb[:, 16 * h : 16 * (h + 1)]), at_n2[0][:, cols], ALU.add
+            )
         denominator(1)
         numerator(0)
         numerator(1)
@@ -218,7 +230,7 @@ def tile_picked_candodds_none_p_kernel(
             numerator(t)
 
         out_rows = out.rearrange("(p t) n -> p t n", t=PACK)
-        pieces = [(t, 0, S) for t in range(last)] + [(last, 0, HALF), (last, HALF, S)]
+        pieces = [(t, 0, S) for t in range(last)] + [(last, 0, 384), (last, 384, S)]
         for t, lo, hi in pieces:
             logs = sbuf("logs%d_%d" % (t, lo), [P, 2, hi - lo], F32)
             nc.scalar.activation(out=logs[:], in_=pairs[t][:, :, lo:hi], func=ACT.Ln)

@@ -152,34 +152,34 @@ def tile_picked_candodds_none_p_kernel(
 
         last = PACK - 1
         pairs = [sbuf("pair%d" % t, [P, 2, S], F32) for t in range(PACK)]
-        ex_copy = [pairs[t + 2][:, 1, :] for t in range(2)] + [sbuf("ex_copy%d" % t, [P, S], F32)[:] for t in (2, 3)]
+        ex_copy = [pairs[2][:, 1, :], pairs[3][:, 1, :], pairs[3][:, 0, :], sbuf("ex_copy_last", [P, S], F32)[:]]
         at_n2 = [
             keep.tile([P, S], F32, name="at_n2_%d" % t, tag="at_n2_%d" % t, align_bytes=64) for t in range(PACK)
         ]
-        shared = psum.tile([P, 2, HALF], F32, name="shared")
-        sums = {(1, 0): shared[:, 0, :], (0, last): shared[:, 1, :]}
 
-        def scores(h, t):
-            if (h, t) not in sums:
-                tag = "sums%d" % t if h == 0 else "hidden%d" % (t - 1)
-                sums.setdefault((h, t), psum.tile([P, HALF], F32, name="sums%d%d" % (h, t), tag=tag)[:])
+        def bank(name, tag, width):
+            return psum.tile([P, width], F32, name=name, tag=tag)
+
+        def scores(dest, t, lo, hi):
+            h, cols = lo // HALF, slice(lo % HALF, (hi - 1) % HALF + 1)
             nc.tensor.matmul_mx(
-                out=sums[(h, t)],
+                out=dest,
                 lhsT=dealt_words[:, t, :].bitcast(FP8X4),
                 lhsT_scale=dealt_scales[:, t, :],
-                rhs=z_codes[h][:].bitcast(FP8X4),
-                rhs_scale=z_scales[h][:],
+                rhs=z_codes[h][:, cols].bitcast(FP8X4),
+                rhs_scale=z_scales[h][:, cols],
                 start=True,
                 stop=True,
             )
 
-        def exponentiate(h, t):
-            cols = slice(h * HALF, (h + 1) * HALF)
-            nc.scalar.activation(out=ex[t][:, cols], in_=sums[(h, t)], func=ACT.Exp, scale=EXP_SCALE)
-            nc.sync.dma_start(out=ex_copy[t][:, cols], in_=ex[t][:, cols])
+        def exponentiate(source, t, lo, hi):
+            nc.scalar.activation(out=ex[t][:, lo:hi], in_=source, func=ACT.Exp, scale=EXP_SCALE)
 
-        def fetch_n2_on_scalar(t):
-            nc.scalar.copy(out=score[t][:, HALF:S], in_=sums[(1, t)])
+        def duplicate(t, lo, hi):
+            nc.sync.dma_start(out=ex_copy[t][:, lo:hi], in_=ex[t][:, lo:hi])
+
+        def fetch_n2_on_scalar(t, source, lo):
+            nc.scalar.copy(out=score[t][:, lo:S], in_=source)
             nc.scalar.activation(out=at_n2[t][:], in_=score[t][:].indirect(n2_sb[:]), func=ACT.Exp, scale=EXP_SCALE)
 
         weigh_on_scalar(2)
@@ -187,29 +187,39 @@ def tile_picked_candodds_none_p_kernel(
         weigh(1)
         quantize_z(0)
         quantize_z(1)
-        for t in range(last):
-            scores(0, t)
+        front = [bank("front%d" % t, "front%d" % t, HALF if t < 2 else S) for t in range(PACK)]
+        for t in range(PACK):
+            scores(front[t][:, :HALF], t, 0, HALF)
         weigh(3)
         quantize_z(2)
         quantize_z(3)
-        for t in range(last):
-            exponentiate(0, t)
-        for t in range(PACK):
-            scores(1, t)
+        for t in range(2):
+            exponentiate(front[t][:], t, 0, HALF)
+            duplicate(t, 0, HALF)
         for t in (1, 2):
-            nc.vector.tensor_copy(score[t][:, :HALF], sums[(0, t)])
-        exponentiate(1, 0)
-        scores(0, last)
+            nc.vector.tensor_copy(score[t][:, :HALF], front[t][:, :HALF])
+        for c in (2, 3):
+            quarter = bank("quarter%d" % c, "hidden%d" % (4 - c), CHUNK)
+            scores(quarter[:], 0, c * CHUNK, (c + 1) * CHUNK)
+            exponentiate(quarter[:], 0, c * CHUNK, (c + 1) * CHUNK)
+        duplicate(0, HALF, S)
+        back = bank("back", "hidden0", HALF)
+        scores(back[:], 1, HALF, S)
+        for t in (2, 3):
+            scores(front[t][:, HALF:], t, HALF, S)
         for h in range(2):
             nc.vector.tensor_copy(at_n2[0][:, h * HALF : (h + 1) * HALF], ex[0][:].indirect(n2_sb[:, 16 * h : 16 * (h + 1)]))
-        exponentiate(1, 1)
-        fetch_n2_on_scalar(1)
-        exponentiate(1, 2)
-        exponentiate(0, last)
-        exponentiate(1, last)
-        fetch_n2_on_scalar(2)
-        nc.scalar.copy(out=score[last][:, :HALF], in_=sums[(0, last)])
-        fetch_n2_on_scalar(last)
+        exponentiate(back[:], 1, HALF, S)
+        duplicate(1, HALF, S)
+        fetch_n2_on_scalar(1, back[:], HALF)
+        for t in (2, 3):
+            exponentiate(front[t][:], t, 0, S)
+            duplicate(t, 0, S if t < last else HALF)
+        fetch_n2_on_scalar(2, front[2][:, HALF:], HALF)
+        fetch_n2_on_scalar(last, front[last][:], 0)
+        nc.scalar.activation(
+            out=ex_copy[last][:, HALF:], in_=score[last][:].indirect(n1_sb[:, 16:]), func=ACT.Exp, scale=EXP_SCALE
+        )
 
         def numerator(t):
             nc.vector.tensor_tensor(pairs[t][:, 0, :], ex[t][:].indirect(n1_sb[:]), ex_copy[t], ALU.add)
@@ -225,12 +235,16 @@ def tile_picked_candodds_none_p_kernel(
         denominator(1)
         numerator(0)
         numerator(1)
-        for t in range(2, PACK):
-            denominator(t)
-            numerator(t)
+        denominator(2)
+        numerator(2)
+        denominator(last)
+        nc.vector.tensor_tensor(
+            pairs[last][:, 0, :HALF], ex[last][:].indirect(n1_sb[:, :16]), ex_copy[last][:, :HALF], ALU.add
+        )
+        nc.vector.tensor_tensor(pairs[last][:, 0, HALF:], ex[last][:, HALF:S], ex_copy[last][:, HALF:], ALU.add)
 
         out_rows = out.rearrange("(p t) n -> p t n", t=PACK)
-        pieces = [(t, 0, S) for t in range(last)] + [(last, 0, 384), (last, 384, S)]
+        pieces = [(t, 0, S) for t in range(last)] + [(last, 0, 320), (last, 320, S)]
         for t, lo, hi in pieces:
             logs = sbuf("logs%d_%d" % (t, lo), [P, 2, hi - lo], F32)
             nc.scalar.activation(out=logs[:], in_=pairs[t][:, :, lo:hi], func=ACT.Ln)

@@ -17,10 +17,17 @@ ACT = mybir.ActivationFunctionType
 
 P = 128
 PACK = 4
+LAST = PACK - 1
+GROUP = 16
+QUADRANT = 32
+LINE = 16
 CHUNK = 128
-HALF = 256
-WINDOW = 1024
+HALF = S // 2
+WINDOW = 2 * S
 EXP_SCALE = 0.5 * 0.0625
+W_PARTS = ((0, 256), (256, 384), (384, 512))
+SCALAR_CHUNK = 2
+LAST_SPLIT = 320
 
 
 def tile_picked_candodds_none_p_kernel(
@@ -31,21 +38,25 @@ def tile_picked_candodds_none_p_kernel(
         keep = ctx.enter_context(tc.tile_pool(name="keep", bufs=1))
         psum = ctx.enter_context(tc.psum_pool(name="psum", bufs=1))
 
-        def sbuf(name, shape, dtype):
-            return keep.tile(shape, dtype, name=name, align_bytes=64)
+        def sbuf(name, shape, dtype, tag=None):
+            return keep.tile(shape, dtype, name=name, tag=tag or name, align_bytes=64)
+
+        def entries(places, lo, hi):
+            return places[:, lo // GROUP : hi // GROUP]
 
         table_words = sbuf("table_words", [P, T], I32)
         table_scales = sbuf("table_scales", [P, T], U8)
-        offs_sb = sbuf("offs_sb", [P, S // 16], U16)
-        cand_sb = sbuf("cand_sb", [P, C // 16], U16)
-        n1_sb = sbuf("n1_sb", [P, S // 16], U16)
-        n2_sb = sbuf("n2_sb", [P, S // 16], U16)
-        n3_sb = sbuf("n3_sb", [P, S // 16], U16)
-        w_parts = [(0, 256), (256, 384), (384, 512)]
-        spare = [S, S, PACK * 256, PACK * 128]
+        offs_sb = sbuf("offs_sb", [P, S // GROUP], U16)
+        cand_sb = sbuf("cand_sb", [P, C // GROUP], U16)
+        n1_sb = sbuf("n1_sb", [P, S // GROUP], U16)
+        n2_sb = sbuf("n2_sb", [P, S // GROUP], U16)
+        n3_sb = sbuf("n3_sb", [P, S // GROUP], U16)
+
+        w_widths = [hi - lo for lo, hi in W_PARTS]
+        spare = [S, S, PACK * w_widths[0], PACK * w_widths[1]]
         ex = [sbuf("ex%d" % t, [P, S + spare[t]], F32) for t in range(PACK)]
-        w_raw = [ex[a + 2][:, S:].rearrange("p (j c) -> p j c", j=PACK) for a in range(2)]
-        w_raw.append(keep.tile([P, PACK, 128], F32, name="w_last", tag="after_cast", align_bytes=64)[:])
+        w_raw = [ex[t][:, S:].rearrange("p (j c) -> p j c", j=PACK) for t in (2, 3)]
+        w_raw.append(sbuf("w_last", [P, PACK, w_widths[2]], F32, tag="after_cast")[:])
         gs_sb = sbuf("gs_sb", [P, PACK], F32)
 
         nc.vector.memset(table_scales[:].bitcast(I32), 0)
@@ -53,14 +64,14 @@ def tile_picked_candodds_none_p_kernel(
         nc.sync.dma_start(offs_sb[:], offs)
         nc.sync.dma_start(cand_sb[:], cand)
         w_rows = w1.rearrange("(p j) c -> p j c", j=PACK)
-        nc.sync.dma_start(out=w_raw[0], in_=w_rows[:, :, :HALF])
-        for q in range(4):
+        nc.sync.dma_start(out=w_raw[0], in_=w_rows[:, :, W_PARTS[0][0] : W_PARTS[0][1]])
+        for q in range(P // QUADRANT):
             nc.sync.dma_start(
-                out=table_scales[32 * q : 32 * q + 4, :].bitcast(I32),
+                out=table_scales[QUADRANT * q : QUADRANT * q + 4, :].bitcast(I32),
                 in_=x_scales[0, 4 * q : 4 * q + 4, :].bitcast(I32),
             )
         for a in (1, 2):
-            nc.sync.dma_start(out=w_raw[a], in_=w_rows[:, :, w_parts[a][0] : w_parts[a][1]])
+            nc.sync.dma_start(out=w_raw[a], in_=w_rows[:, :, W_PARTS[a][0] : W_PARTS[a][1]])
         nc.sync.dma_start(out=gs_sb[:], in_=gs.rearrange("(p t) o -> p (t o)", t=PACK))
         nc.sync.dma_start(n2_sb[:], n2)
         nc.sync.dma_start(n3_sb[:], n3)
@@ -69,11 +80,9 @@ def tile_picked_candodds_none_p_kernel(
         score = {t: sbuf("score%d" % t, [P, WINDOW], F32) for t in range(1, PACK)}
         for window in (ex[0], ex[1], score[1], score[2]):
             nc.vector.memset(window[:, S:], 0.0)
-        warm = sbuf("warm", [P, 1], F32)
-        nc.scalar.activation(out=warm[:], in_=ex[0][:, S : S + 1], func=ACT.Exp)
 
-        w_grouped = keep.tile([P, PACK, P, PACK], BF16, name="w_grouped", tag="after_w", align_bytes=64)
-        for a, (lo, hi) in enumerate(w_parts):
+        w_grouped = sbuf("w_grouped", [P, PACK, P, PACK], BF16, tag="after_w")
+        for a, (lo, hi) in enumerate(W_PARTS):
             nc.scalar.copy(
                 out=w_grouped[:, :, lo // PACK : hi // PACK, :].rearrange("p t m j -> p m j t"),
                 in_=w_raw[a].rearrange("p j (m t) -> p m j t", t=PACK),
@@ -93,17 +102,18 @@ def tile_picked_candodds_none_p_kernel(
         nc.vector.quantize_mx(
             out=w_codes[:].bitcast(FP8X4), scales=w_scales[:], in_=w_grouped[:].rearrange("p t m j -> p (t m j)")
         )
-        cand_scales = keep.tile([P, C], U8, name="cand_scales", tag="after_cast", align_bytes=64)
+        cand_scales = sbuf("cand_scales", [P, C], U8, tag="after_cast")
         nc.vector.tensor_copy(cand_scales[:], table_scales[:].indirect(cand_sb[:]))
-        dealt_words = keep.tile([P, PACK, P], U32, name="dealt_words", tag="after_w", align_bytes=64)
-        for dealt, picked, run in ((dealt_words, cand_words, 4), (dealt_scales, cand_scales, 16)):
+        dealt_words = sbuf("dealt_words", [P, PACK, P], U32, tag="after_w")
+        for dealt, picked, run in ((dealt_words, cand_words, LINE // 4), (dealt_scales, cand_scales, LINE)):
             nc.vector.tensor_copy(
                 dealt[:].rearrange("p t (g i) -> p g t i", i=run),
                 picked[:].rearrange("p (g i t) -> p g t i", i=run, t=PACK),
             )
 
-        hidden = [psum.tile([P, PACK, CHUNK], F32, name="hidden%d" % c) for c in range(4)]
-        for c in (2, 0, 1, 3):
+        chunks = range(S // CHUNK)
+        hidden = [psum.tile([P, PACK, CHUNK], F32, name="hidden%d" % c) for c in chunks]
+        for c in [SCALAR_CHUNK] + [c for c in chunks if c != SCALAR_CHUNK]:
             cols = slice(c * CHUNK, (c + 1) * CHUNK)
             for t in range(PACK):
                 nc.tensor.matmul_mx(
@@ -133,13 +143,13 @@ def tile_picked_candodds_none_p_kernel(
             )
 
         def weigh_on_scalar(c):
-            positive = score[PACK - 1][:, S:].rearrange("p (t n) -> p t n", t=PACK)
+            positive = score[LAST][:, S:].rearrange("p (t n) -> p t n", t=PACK)
             nc.scalar.activation(out=positive, in_=hidden[c][:], func=ACT.Relu)
-            planes = score[2][:, :HALF].bitcast(BF16).rearrange("p (t n) -> p t n", t=PACK)
+            rounded = score[2][:, :HALF].bitcast(BF16).rearrange("p (t n) -> p t n", t=PACK)
             for t in range(PACK):
-                nc.scalar.activation(out=planes[:, t, :], in_=positive[:, t, :], func=ACT.Copy, scale=gs_sb[:, t : t + 1])
+                nc.scalar.activation(out=rounded[:, t, :], in_=positive[:, t, :], func=ACT.Copy, scale=gs_sb[:, t : t + 1])
             nc.scalar.copy(
-                out=z[c].rearrange("p (g i) t -> p g t i", i=4), in_=planes.rearrange("p t (g i) -> p g t i", i=4)
+                out=z[c].rearrange("p (g i) t -> p g t i", i=4), in_=rounded.rearrange("p t (g i) -> p g t i", i=4)
             )
 
         def quantize_z(c):
@@ -150,12 +160,9 @@ def tile_picked_candodds_none_p_kernel(
                 in_=z[c].rearrange("p n t -> p (n t)"),
             )
 
-        last = PACK - 1
         pairs = [sbuf("pair%d" % t, [P, 2, S], F32) for t in range(PACK)]
-        ex_copy = [pairs[2][:, 1, :], pairs[3][:, 1, :], pairs[3][:, 0, :], sbuf("ex_copy_last", [P, S], F32)[:]]
-        at_n2 = [
-            keep.tile([P, S], F32, name="at_n2_%d" % t, tag="at_n2_%d" % t, align_bytes=64) for t in range(PACK)
-        ]
+        addend = [pairs[2][:, 1, :], pairs[3][:, 1, :], pairs[3][:, 0, :], sbuf("ex_copy_last", [P, S], F32)[:]]
+        at_n2 = [sbuf("at_n2_%d" % t, [P, S], F32) for t in range(PACK)]
 
         def bank(name, tag, width):
             return psum.tile([P, width], F32, name=name, tag=tag)
@@ -176,13 +183,13 @@ def tile_picked_candodds_none_p_kernel(
             nc.scalar.activation(out=ex[t][:, lo:hi], in_=source, func=ACT.Exp, scale=EXP_SCALE)
 
         def duplicate(t, lo, hi):
-            nc.sync.dma_start(out=ex_copy[t][:, lo:hi], in_=ex[t][:, lo:hi])
+            nc.sync.dma_start(out=addend[t][:, lo:hi], in_=ex[t][:, lo:hi])
 
         def fetch_n2_on_scalar(t, source, lo):
             nc.scalar.copy(out=score[t][:, lo:S], in_=source)
             nc.scalar.activation(out=at_n2[t][:], in_=score[t][:].indirect(n2_sb[:]), func=ACT.Exp, scale=EXP_SCALE)
 
-        weigh_on_scalar(2)
+        weigh_on_scalar(SCALAR_CHUNK)
         weigh(0)
         weigh(1)
         quantize_z(0)
@@ -198,8 +205,8 @@ def tile_picked_candodds_none_p_kernel(
             duplicate(t, 0, HALF)
         for t in (1, 2):
             nc.vector.tensor_copy(score[t][:, :HALF], front[t][:, :HALF])
-        for c in (2, 3):
-            quarter = bank("quarter%d" % c, "hidden%d" % (4 - c), CHUNK)
+        for c, tag in ((2, "hidden2"), (3, "hidden1")):
+            quarter = bank("quarter%d" % c, tag, CHUNK)
             scores(quarter[:], 0, c * CHUNK, (c + 1) * CHUNK)
             exponentiate(quarter[:], 0, c * CHUNK, (c + 1) * CHUNK)
         duplicate(0, HALF, S)
@@ -207,48 +214,51 @@ def tile_picked_candodds_none_p_kernel(
         scores(back[:], 1, HALF, S)
         for t in (2, 3):
             scores(front[t][:, HALF:], t, HALF, S)
-        for h in range(2):
-            nc.vector.tensor_copy(at_n2[0][:, h * HALF : (h + 1) * HALF], ex[0][:].indirect(n2_sb[:, 16 * h : 16 * (h + 1)]))
+
+        halves = ((0, HALF), (HALF, S))
+        for lo, hi in halves:
+            nc.vector.tensor_copy(at_n2[0][:, lo:hi], ex[0][:].indirect(entries(n2_sb, lo, hi)))
         exponentiate(back[:], 1, HALF, S)
         duplicate(1, HALF, S)
         fetch_n2_on_scalar(1, back[:], HALF)
         for t in (2, 3):
             exponentiate(front[t][:], t, 0, S)
-            duplicate(t, 0, S if t < last else HALF)
+            duplicate(t, 0, S if t < LAST else HALF)
         fetch_n2_on_scalar(2, front[2][:, HALF:], HALF)
-        fetch_n2_on_scalar(last, front[last][:], 0)
+        fetch_n2_on_scalar(LAST, front[LAST][:], 0)
         nc.scalar.activation(
-            out=ex_copy[last][:, HALF:], in_=score[last][:].indirect(n1_sb[:, 16:]), func=ACT.Exp, scale=EXP_SCALE
+            out=addend[LAST][:, HALF:],
+            in_=score[LAST][:].indirect(entries(n1_sb, HALF, S)),
+            func=ACT.Exp,
+            scale=EXP_SCALE,
         )
 
-        def numerator(t):
-            nc.vector.tensor_tensor(pairs[t][:, 0, :], ex[t][:].indirect(n1_sb[:]), ex_copy[t], ALU.add)
-
-        def denominator(t):
-            nc.vector.tensor_tensor(pairs[t][:, 1, :], ex[t][:].indirect(n3_sb[:]), at_n2[t][:], ALU.add)
-
-        for h in range(2):
-            cols = slice(h * HALF, (h + 1) * HALF)
+        def numerator(t, lo=0, hi=S):
             nc.vector.tensor_tensor(
-                pairs[0][:, 1, cols], ex[0][:].indirect(n3_sb[:, 16 * h : 16 * (h + 1)]), at_n2[0][:, cols], ALU.add
+                pairs[t][:, 0, lo:hi], ex[t][:].indirect(entries(n1_sb, lo, hi)), addend[t][:, lo:hi], ALU.add
             )
+
+        def denominator(t, lo=0, hi=S):
+            nc.vector.tensor_tensor(
+                pairs[t][:, 1, lo:hi], ex[t][:].indirect(entries(n3_sb, lo, hi)), at_n2[t][:, lo:hi], ALU.add
+            )
+
+        for lo, hi in halves:
+            denominator(0, lo, hi)
         denominator(1)
         numerator(0)
         numerator(1)
         denominator(2)
         numerator(2)
-        denominator(last)
-        nc.vector.tensor_tensor(
-            pairs[last][:, 0, :HALF], ex[last][:].indirect(n1_sb[:, :16]), ex_copy[last][:, :HALF], ALU.add
-        )
-        nc.vector.tensor_tensor(pairs[last][:, 0, HALF:], ex[last][:, HALF:S], ex_copy[last][:, HALF:], ALU.add)
+        denominator(LAST)
+        numerator(LAST, 0, HALF)
+        nc.vector.tensor_tensor(pairs[LAST][:, 0, HALF:], ex[LAST][:, HALF:S], addend[LAST][:, HALF:], ALU.add)
 
         out_rows = out.rearrange("(p t) n -> p t n", t=PACK)
-        pieces = [(t, 0, S) for t in range(last)] + [(last, 0, 320), (last, 320, S)]
+        pieces = [(t, 0, S) for t in range(LAST)] + [(LAST, 0, LAST_SPLIT), (LAST, LAST_SPLIT, S)]
         for t, lo, hi in pieces:
             logs = sbuf("logs%d_%d" % (t, lo), [P, 2, hi - lo], F32)
             nc.scalar.activation(out=logs[:], in_=pairs[t][:, :, lo:hi], func=ACT.Ln)
-            tag = "at_n2_%d" % last if t == 0 else "odds%d_%d" % (t, lo)
-            odds = keep.tile([P, hi - lo], F32, name="odds%d_%d" % (t, lo), tag=tag, align_bytes=64)
+            odds = sbuf("odds%d_%d" % (t, lo), [P, hi - lo], F32, tag="at_n2_%d" % LAST if t == 0 else None)
             nc.vector.tensor_tensor(odds[:], logs[:, 0, :], logs[:, 1, :], ALU.subtract)
             nc.sync.dma_start(out=out_rows[:, t, lo:hi], in_=odds[:])

from contextlib import ExitStack

import concourse.mybir as mybir

K, T, S, H, C = 512, 2048, 512, 512, 512
FLOPS = 2 * K * H * S + 2 * H * C * S

F32 = mybir.dt.float32
BF16 = mybir.dt.bfloat16
I32 = mybir.dt.int32
U32 = mybir.dt.uint32
U16 = mybir.dt.uint16
U8 = mybir.dt.uint8
FP8X4 = mybir.dt.float8_e4m3fn_x4
ALU = mybir.AluOpType
ACT = mybir.ActivationFunctionType

P = 128
PACK = 4
LAST = PACK - 1
GROUP = 16
QUADRANT = 32
LINE = 16
CHUNK = 128
HALF = S // 2
WINDOW = 2 * S
EXP_SCALE = 0.5 * 0.0625
W_PARTS = ((0, 256), (256, 384), (384, 512))
SCALAR_CHUNK = 2
LAST_SPLIT = 320


def tile_picked_candodds_none_p_kernel(
    tc, x_words, x_scales, w1, gs, offs, cand, n1, n2, n3, out
):
    nc = tc.nc
    with ExitStack() as ctx:
        keep = ctx.enter_context(tc.tile_pool(name="keep", bufs=1))
        psum = ctx.enter_context(tc.psum_pool(name="psum", bufs=1))

        def sbuf(name, shape, dtype, tag=None):
            return keep.tile(shape, dtype, name=name, tag=tag or name, align_bytes=64)

        def entries(places, lo, hi):
            return places[:, lo // GROUP : hi // GROUP]

        table_words = sbuf("table_words", [P, T], I32)
        table_scales = sbuf("table_scales", [P, T], U8)
        offs_sb = sbuf("offs_sb", [P, S // GROUP], U16)
        cand_sb = sbuf("cand_sb", [P, C // GROUP], U16)
        n1_sb = sbuf("n1_sb", [P, S // GROUP], U16)
        n2_sb = sbuf("n2_sb", [P, S // GROUP], U16)
        n3_sb = sbuf("n3_sb", [P, S // GROUP], U16)

        w_widths = [hi - lo for lo, hi in W_PARTS]
        spare = [S, S, PACK * w_widths[0], PACK * w_widths[1]]
        ex = [sbuf("ex%d" % t, [P, S + spare[t]], F32) for t in range(PACK)]
        w_raw = [ex[t][:, S:].rearrange("p (j c) -> p j c", j=PACK) for t in (2, 3)]
        w_raw.append(sbuf("w_last", [P, PACK, w_widths[2]], F32, tag="after_cast")[:])
        gs_sb = sbuf("gs_sb", [P, PACK], F32)

        nc.vector.memset(table_scales[:].bitcast(I32), 0)
        nc.sync.dma_start(out=table_words[:], in_=x_words[0].rearrange("p n t -> p (n t)").bitcast(I32))
        nc.sync.dma_start(offs_sb[:], offs)
        nc.sync.dma_start(cand_sb[:], cand)
        w_rows = w1.rearrange("(p j) c -> p j c", j=PACK)
        nc.sync.dma_start(out=w_raw[0], in_=w_rows[:, :, W_PARTS[0][0] : W_PARTS[0][1]])
        for q in range(P // QUADRANT):
            nc.sync.dma_start(
                out=table_scales[QUADRANT * q : QUADRANT * q + 4, :].bitcast(I32),
                in_=x_scales[0, 4 * q : 4 * q + 4, :].bitcast(I32),
            )
        for a in (1, 2):
            nc.sync.dma_start(out=w_raw[a], in_=w_rows[:, :, W_PARTS[a][0] : W_PARTS[a][1]])
        nc.sync.dma_start(out=gs_sb[:], in_=gs.rearrange("(p t) o -> p (t o)", t=PACK))
        nc.sync.dma_start(n2_sb[:], n2)
        nc.sync.dma_start(n3_sb[:], n3)
        nc.sync.dma_start(n1_sb[:], n1)

        score = {t: sbuf("score%d" % t, [P, WINDOW], F32) for t in range(1, PACK)}
        for window in (ex[0], ex[1], score[1], score[2]):
            nc.vector.memset(window[:, S:], 0.0)

        w_grouped = sbuf("w_grouped", [P, PACK, P, PACK], BF16, tag="after_w")
        for a, (lo, hi) in enumerate(W_PARTS):
            nc.scalar.copy(
                out=w_grouped[:, :, lo // PACK : hi // PACK, :].rearrange("p t m j -> p m j t"),
                in_=w_raw[a].rearrange("p j (m t) -> p m j t", t=PACK),
            )

        tok_words = sbuf("tok_words", [P, S], U32)
        tok_scales = sbuf("tok_scales", [P, S], U8)
        cand_words = sbuf("cand_words", [P, C], U32)
        dealt_scales = sbuf("dealt_scales", [P, PACK, P], U8)
        w_codes = sbuf("w_codes", [P, H], U32)
        w_scales = sbuf("w_scales", [P, H], U8)

        words_window = table_words[:].bitcast(U32)
        nc.vector.tensor_copy(tok_words[:], words_window.indirect(offs_sb[:]))
        nc.vector.tensor_copy(cand_words[:], words_window.indirect(cand_sb[:]))
        nc.vector.tensor_copy(tok_scales[:], table_scales[:].indirect(offs_sb[:]))
        nc.vector.quantize_mx(
            out=w_codes[:].bitcast(FP8X4), scales=w_scales[:], in_=w_grouped[:].rearrange("p t m j -> p (t m j)")
        )
        cand_scales = sbuf("cand_scales", [P, C], U8, tag="after_cast")
        nc.vector.tensor_copy(cand_scales[:], table_scales[:].indirect(cand_sb[:]))
        dealt_words = sbuf("dealt_words", [P, PACK, P], U32, tag="after_w")
        for dealt, picked, run in ((dealt_words, cand_words, LINE // 4), (dealt_scales, cand_scales, LINE)):
            nc.vector.tensor_copy(
                dealt[:].rearrange("p t (g i) -> p g t i", i=run),
                picked[:].rearrange("p (g i t) -> p g t i", i=run, t=PACK),
            )

        chunks = range(S // CHUNK)
        hidden = [psum.tile([P, PACK, CHUNK], F32, name="hidden%d" % c) for c in chunks]
        for c in [SCALAR_CHUNK] + [c for c in chunks if c != SCALAR_CHUNK]:
            cols = slice(c * CHUNK, (c + 1) * CHUNK)
            for t in range(PACK):
                nc.tensor.matmul_mx(
                    out=hidden[c][:, t, :],
                    lhsT=w_codes[:, t * P : (t + 1) * P].bitcast(FP8X4),
                    lhsT_scale=w_scales[:, t * P : (t + 1) * P],
                    rhs=tok_words[:, cols].bitcast(FP8X4),
                    rhs_scale=tok_scales[:, cols],
                    start=True,
                    stop=True,
                )

        z = [sbuf("z%d" % c, [P, CHUNK, PACK], BF16)[:] for c in (0, 1)]
        z.extend([score[1][:, :HALF].bitcast(BF16).rearrange("p (n t) -> p n t", t=PACK), z[0]])
        z_codes = [sbuf("z_codes%d" % h, [P, HALF], U32) for h in range(2)]
        z_scales = [sbuf("z_scales%d" % h, [P, HALF], U8) for h in range(2)]
        gs_spread = gs_sb[:].unsqueeze(1).to_broadcast([P, CHUNK, PACK])

        def weigh(c):
            nc.vector.scalar_tensor_tensor(
                out=z[c],
                in0=hidden[c][:].rearrange("p t n -> p n t"),
                scalar=0.0,
                in1=gs_spread,
                op0=ALU.max,
                op1=ALU.mult,
            )

        def weigh_on_scalar(c):
            positive = score[LAST][:, S:].rearrange("p (t n) -> p t n", t=PACK)
            nc.scalar.activation(out=positive, in_=hidden[c][:], func=ACT.Relu)
            rounded = score[2][:, :HALF].bitcast(BF16).rearrange("p (t n) -> p t n", t=PACK)
            for t in range(PACK):
                nc.scalar.activation(out=rounded[:, t, :], in_=positive[:, t, :], func=ACT.Copy, scale=gs_sb[:, t : t + 1])
            nc.scalar.copy(
                out=z[c].rearrange("p (g i) t -> p g t i", i=4), in_=rounded.rearrange("p t (g i) -> p g t i", i=4)
            )

        def quantize_z(c):
            cols = slice((c % 2) * CHUNK, (c % 2 + 1) * CHUNK)
            nc.vector.quantize_mx(
                out=z_codes[c // 2][:, cols].bitcast(FP8X4),
                scales=z_scales[c // 2][:, cols],
                in_=z[c].rearrange("p n t -> p (n t)"),
            )

        pairs = [sbuf("pair%d" % t, [P, 2, S], F32) for t in range(PACK)]
        addend = [pairs[2][:, 1, :], pairs[3][:, 1, :], pairs[3][:, 0, :], sbuf("ex_copy_last", [P, S], F32)[:]]
        at_n2 = [sbuf("at_n2_%d" % t, [P, S], F32) for t in range(PACK)]

        def bank(name, tag, width):
            return psum.tile([P, width], F32, name=name, tag=tag)

        def scores(dest, t, lo, hi):
            h, cols = lo // HALF, slice(lo % HALF, (hi - 1) % HALF + 1)
            nc.tensor.matmul_mx(
                out=dest,
                lhsT=dealt_words[:, t, :].bitcast(FP8X4),
                lhsT_scale=dealt_scales[:, t, :],
                rhs=z_codes[h][:, cols].bitcast(FP8X4),
                rhs_scale=z_scales[h][:, cols],
                start=True,
                stop=True,
            )

        def exponentiate(source, t, lo, hi):
            nc.scalar.activation(out=ex[t][:, lo:hi], in_=source, func=ACT.Exp, scale=EXP_SCALE)

        def duplicate(t, lo, hi):
            nc.sync.dma_start(out=addend[t][:, lo:hi], in_=ex[t][:, lo:hi])

        def fetch_n2_on_scalar(t, source, lo):
            nc.scalar.copy(out=score[t][:, lo:S], in_=source)
            nc.scalar.activation(out=at_n2[t][:], in_=score[t][:].indirect(n2_sb[:]), func=ACT.Exp, scale=EXP_SCALE)

        weigh_on_scalar(SCALAR_CHUNK)
        weigh(0)
        weigh(1)
        quantize_z(0)
        quantize_z(1)
        front = [bank("front%d" % t, "front%d" % t, HALF if t < 2 else S) for t in range(PACK)]
        for t in range(PACK):
            scores(front[t][:, :HALF], t, 0, HALF)
        weigh(3)
        quantize_z(2)
        quantize_z(3)
        for t in range(2):
            exponentiate(front[t][:], t, 0, HALF)
            duplicate(t, 0, HALF)
        for t in (1, 2):
            nc.vector.tensor_copy(score[t][:, :HALF], front[t][:, :HALF])
        for c, tag in ((2, "hidden2"), (3, "hidden1")):
            quarter = bank("quarter%d" % c, tag, CHUNK)
            scores(quarter[:], 0, c * CHUNK, (c + 1) * CHUNK)
            exponentiate(quarter[:], 0, c * CHUNK, (c + 1) * CHUNK)
        duplicate(0, HALF, S)
        back = bank("back", "hidden0", HALF)
        scores(back[:], 1, HALF, S)
        for t in (2, 3):
            scores(front[t][:, HALF:], t, HALF, S)

        halves = ((0, HALF), (HALF, S))
        for lo, hi in halves:
            nc.vector.tensor_copy(at_n2[0][:, lo:hi], ex[0][:].indirect(entries(n2_sb, lo, hi)))
        exponentiate(back[:], 1, HALF, S)
        duplicate(1, HALF, S)
        fetch_n2_on_scalar(1, back[:], HALF)
        for t in (2, 3):
            exponentiate(front[t][:], t, 0, S)
            duplicate(t, 0, S if t < LAST else HALF)
        fetch_n2_on_scalar(2, front[2][:, HALF:], HALF)
        fetch_n2_on_scalar(LAST, front[LAST][:], 0)
        nc.scalar.activation(
            out=addend[LAST][:, HALF:],
            in_=score[LAST][:].indirect(entries(n1_sb, HALF, S)),
            func=ACT.Exp,
            scale=EXP_SCALE,
        )

        def numerator(t, lo=0, hi=S):
            nc.vector.tensor_tensor(
                pairs[t][:, 0, lo:hi], ex[t][:].indirect(entries(n1_sb, lo, hi)), addend[t][:, lo:hi], ALU.add
            )

        def denominator(t, lo=0, hi=S):
            nc.vector.tensor_tensor(
                pairs[t][:, 1, lo:hi], ex[t][:].indirect(entries(n3_sb, lo, hi)), at_n2[t][:, lo:hi], ALU.add
            )

        for lo, hi in halves:
            denominator(0, lo, hi)
        denominator(1)
        numerator(0)
        numerator(1)
        denominator(2)
        numerator(2)
        denominator(LAST)
        numerator(LAST, 0, HALF)
        nc.vector.tensor_tensor(pairs[LAST][:, 0, HALF:], ex[LAST][:, HALF:S], addend[LAST][:, HALF:], ALU.add)

        out_rows = out.rearrange("(p t) n -> p t n", t=PACK)
        pieces = [(t, 0, S) for t in range(LAST)] + [(LAST, 0, LAST_SPLIT), (LAST, LAST_SPLIT, S)]
        for t, lo, hi in pieces:
            logs = sbuf("logs%d_%d" % (t, lo), [P, 2, hi - lo], F32)
            nc.scalar.activation(out=logs[:], in_=pairs[t][:, :, lo:hi], func=ACT.Ln)
            odds = sbuf("odds%d_%d" % (t, lo), [P, hi - lo], F32, tag="at_n2_%d" % LAST if t == 0 else None)
            nc.vector.tensor_tensor(odds[:], logs[:, 0, :], logs[:, 1, :], ALU.subtract)
            nc.sync.dma_start(out=out_rows[:, t, lo:hi], in_=odds[:])
